import numpy as np, ml_dtypes
CORES = [33,34,161,162,289,290,417,418]
N = 8
GR, GC = 2, 4
L, KA, KB, F = 4, 1, 2, 128
def setup_inputs(rng):
    return {"a": rng.standard_normal((N, 128, KA * 128), dtype=np.float32).astype(ml_dtypes.bfloat16), "b": rng.standard_normal((N, 128, KB * F), dtype=np.float32).astype(ml_dtypes.bfloat16)}
def setup_inputs_big(rng):
    d = setup_inputs(rng)
    for k in ("a", "b"): d[k] = (d[k].astype(np.float32) * 1024.0).astype(d[k].dtype)
    return d
def setup_inputs_small(rng):
    d = setup_inputs(rng)
    for k in ("a", "b"): d[k] = (d[k].astype(np.float32) * (1 / 1024.0)).astype(d[k].dtype)
    return d
def setup_inputs_apart(rng):
    d = setup_inputs(rng)
    f = (10.0 ** rng.permutation(np.linspace(-1.5, 1.5, N))).astype(np.float32).reshape(N, 1, 1)
    for k in ("a", "b"): d[k] = (d[k].astype(np.float32) * f).astype(d[k].dtype)
    return d
def reference(a, b):
    A, B = a.astype(np.float64), b.astype(np.float64)
    y = np.zeros((N, 128, F))
    for i in range(GR):
        for j in range(GC):
            for k in range(L):
                At = A[i * GC + k // KA][:, 128 * (k % KA):128 * (k % KA) + 128]
                Bt = B[(k // KB) * GC + j][:, F * (k % KB):F * (k % KB) + F]
                y[i * GC + j] += At.T @ Bt
    return {"y": y.astype(ml_dtypes.bfloat16 if a.dtype != np.float64 else np.float64)}

@@ -1,0 +1,132 @@
+from concourse.bass import DstId, RemoteDMATransfer
+
+GR, GC, L, KB, F = 2, 4, 4, 2, 128
+
+SCRATCH = {
+    "a_sb": ("sbuf", [128, L * 128], "bfloat16"),
+    "b_sb": ("sbuf", [128, L * F], "bfloat16"),
+    "b_out": ("dram", [128, KB * F], "bfloat16"),
+    "b_rel": ("dram", [128, KB * F], "bfloat16"),
+    "y_sb": ("sbuf", [128, F], "bfloat16"),
+    "acc": ("psum", [128, F], "float32"),
+}
+SEMAPHORES = ["ld_stage", "ld_a", "ld_b", "rel_in", "b_in", "a_in", "sent", "mm", "cp", "st"]
+
+HOP1_ENGINES = 4
+ONCHIP_ENGINES = 4
+
+
+def _bits(mask):
+    return [e for e in range(16) if (mask >> e) & 1]
+
+
+def _mask(engines):
+    m = 0
+    for e in engines:
+        m |= 1 << e
+    return m
+
+
+def _same_chip(topo, a, b):
+    return topo.host(a) == topo.host(b) and topo.chip(a) == topo.chip(b)
+
+
+def _relays(cores, topo):
+    n = len(cores)
+    load = [0] * n
+    relay = []
+    for r in range(n):
+        d = (r + GC) % n
+        cand = [m for m in range(n) if m != r and m != d
+                and topo.may_write(cores[r], cores[m]) and topo.may_write(cores[m], cores[d])
+                and topo.rack(topo.host(cores[m])) == topo.rack(topo.host(cores[d]))]
+        m = min(cand, key=lambda q: (load[q], q))
+        load[m] += 1
+        relay.append(m)
+    return relay
+
+
+def _a_masks(cores, topo, r):
+    src = cores[r]
+    peers = [p for p in range((r // GC) * GC, (r // GC) * GC + GC) if p != r]
+    far = [p for p in peers if not _same_chip(topo, src, cores[p])]
+    near = [p for p in peers if _same_chip(topo, src, cores[p])]
+    out = {}
+    leave = _bits(topo.mask(src, cores[far[0]])) if far else []
+    share = len(leave) // max(1, len(far))
+    for n, p in enumerate(far):
+        out[p] = _mask(leave[n * share:(n + 1) * share])
+    for n, p in enumerate(near):
+        stay = [e for e in _bits(topo.mask(src, cores[p])) if e not in leave]
+        out[p] = _mask(stay[n * ONCHIP_ENGINES:(n + 1) * ONCHIP_ENGINES])
+    return out
+
+
+def rank_program(g, core, T, topo):
+    rank = T.rank_of(core)
+    if rank is None:
+        return
+    cores = list(T.cores)
+    n = len(cores)
+    row, col = rank // GC, rank % GC
+    sem = T.sem
+    relay = _relays(cores, topo)
+    own_k = [KB * row + t for t in range(KB)]
+    far_k = [k for k in range(L) if k not in own_k]
+
+    g.sync.dma_start(T.b_out[:, :], T.b[:, :]).then_inc(sem.ld_stage, 16)
+    g.scalar.dma_start(T.a_sb[:, col * 128:(col + 1) * 128], T.a[:, :]).then_inc(sem.ld_a, 16)
+    g.sync.dma_start(T.b_sb[:, own_k[0] * F:(own_k[-1] + 1) * F], T.b[:, :]).then_inc(sem.ld_b, 16)
+
+    sent = 0
+    m = cores[relay[rank]]
+    hop1 = _bits(topo.mask(core, m))[:HOP1_ENGINES]
+    rid, pid = topo.addr(m, core)
+    g.wait_ge(sem.ld_stage, 16)
+    g.remote_dma(T.b_rel[:, :], T.b_out[:, :], sem.rel_in, sem.sent, pid, rid, _mask(hop1))
+    sent += len(hop1)
+
+    transfers = []
+    for p, mask in _a_masks(cores, topo, rank).items():
+        rid, pid = topo.addr(cores[p], core)
+        blk = T.a_sb[:, col * 128:(col + 1) * 128]
+        transfers.append(RemoteDMATransfer(dst_ids=[DstId(rid=rid, pnc=pid)], dma_engine_mask=mask, remote_sem=sem.a_in,
+                                           src=blk, dst=blk))
+        sent += len(_bits(mask))
+    g.wait_ge(sem.ld_a, 16)
+    g.remote_dma_fused(transfers, local_sem=sem.sent)
+
+    for s in range(n):
+        if relay[s] != rank:
+            continue
+        d = (s + GC) % n
+        got = len(_bits(topo.mask(cores[s], core))[:HOP1_ENGINES])
+        hop2 = _bits(topo.mask(core, cores[d]))
+        rid, pid = topo.addr(cores[d], core)
+        k0 = KB * (s // GC)
+        g.wait_ge(sem.rel_in, got)
+        g.remote_dma(T.b_sb[:, k0 * F:(k0 + KB) * F], T.b_rel[:, :], sem.b_in, sem.sent, pid, rid, _mask(hop2))
+        sent += len(hop2)
+
+    a_total = sum(len(_bits(_a_masks(cores, topo, p)[rank])) for p in range(row * GC, row * GC + GC) if p != rank)
+    partner = (rank + GC) % n
+    b_total = len(_bits(topo.mask(cores[relay[partner]], core)))
+    te = g.tensor
+    te.wait_ge(sem.ld_a, 16)
+    te.wait_ge(sem.ld_b, 16)
+    te.wait_ge(sem.a_in, a_total)
+    for q, k in enumerate(own_k):
+        te.matmul(T.acc[:, :], T.a_sb[:, k * 128:(k + 1) * 128], T.b_sb[:, k * F:(k + 1) * F], start=(q == 0), stop=False)
+    te.wait_ge(sem.b_in, b_total)
+    for q, k in enumerate(far_k):
+        last = q == len(far_k) - 1
+        ins = te.matmul(T.acc[:, :], T.a_sb[:, k * 128:(k + 1) * 128], T.b_sb[:, k * F:(k + 1) * F], start=False, stop=last)
+        if last:
+            ins.then_inc(sem.mm, 1)
+
+    g.vector.wait_ge(sem.mm, 1)
+    g.vector.tensor_copy(T.y_sb[:, :], T.acc[:, :]).then_inc(sem.cp, 1)
+    g.sync.wait_ge(sem.cp, 1)
+    g.sync.dma_start(T.y[:, :], T.y_sb[:, :]).then_inc(sem.st, 16)
+    g.sync.wait_ge(sem.st, 16)
+    g.wait_ge(sem.sent, sent)

@@ -5,12 +5,13 @@ GR, GC, L, KB, F = 2, 4, 4, 2, 128
 SCRATCH = {
     "a_sb": ("sbuf", [128, L * 128], "bfloat16"),
     "b_sb": ("sbuf", [128, L * F], "bfloat16"),
-    "b_out": ("dram", [128, KB * F], "bfloat16"),
-    "b_rel": ("dram", [128, KB * F], "bfloat16"),
+    "b_out": ("dram", [KB, 128, F], "bfloat16"),
+    "b_rel": ("dram", [KB, 128, F], "bfloat16"),
     "y_sb": ("sbuf", [128, F], "bfloat16"),
     "acc": ("psum", [128, F], "float32"),
 }
-SEMAPHORES = ["ld_stage", "ld_a", "ld_b", "rel_in", "b_in", "a_in", "sent", "mm", "cp", "st"]
+SEMAPHORES = (["ld_a", "ld_b", "a_in", "sent", "mm", "cp", "st"]
+              + ["ld_s%d" % t for t in range(KB)] + ["rel%d" % t for t in range(KB)] + ["bin%d" % t for t in range(KB)])
 
 HOP1_ENGINES = 4
 ONCHIP_ENGINES = 4
@@ -74,7 +75,9 @@ def rank_program(g, core, T, topo):
     own_k = [KB * row + t for t in range(KB)]
     far_k = [k for k in range(L) if k not in own_k]
 
-    g.sync.dma_start(T.b_out[:, :], T.b[:, :]).then_inc(sem.ld_stage, 16)
+    queues = [g.sync, g.scalar]
+    for t in range(KB):
+        queues[t % 2].dma_start(T.b_out[t], T.b[:, t * F:(t + 1) * F]).then_inc(sem["ld_s%d" % t], 16)
     g.scalar.dma_start(T.a_sb[:, col * 128:(col + 1) * 128], T.a[:, :]).then_inc(sem.ld_a, 16)
     g.sync.dma_start(T.b_sb[:, own_k[0] * F:(own_k[-1] + 1) * F], T.b[:, :]).then_inc(sem.ld_b, 16)
 
@@ -82,9 +85,10 @@ def rank_program(g, core, T, topo):
     m = cores[relay[rank]]
     hop1 = _bits(topo.mask(core, m))[:HOP1_ENGINES]
     rid, pid = topo.addr(m, core)
-    g.wait_ge(sem.ld_stage, 16)
-    g.remote_dma(T.b_rel[:, :], T.b_out[:, :], sem.rel_in, sem.sent, pid, rid, _mask(hop1))
-    sent += len(hop1)
+    for t in range(KB):
+        g.wait_ge(sem["ld_s%d" % t], 16)
+        g.remote_dma(T.b_rel[t], T.b_out[t], sem["rel%d" % t], sem.sent, pid, rid, _mask(hop1))
+        sent += len(hop1)
 
     transfers = []
     for p, mask in _a_masks(cores, topo, rank).items():
@@ -103,10 +107,11 @@ def rank_program(g, core, T, topo):
         got = len(_bits(topo.mask(cores[s], core))[:HOP1_ENGINES])
         hop2 = _bits(topo.mask(core, cores[d]))
         rid, pid = topo.addr(cores[d], core)
-        k0 = KB * (s // GC)
-        g.wait_ge(sem.rel_in, got)
-        g.remote_dma(T.b_sb[:, k0 * F:(k0 + KB) * F], T.b_rel[:, :], sem.b_in, sem.sent, pid, rid, _mask(hop2))
-        sent += len(hop2)
+        for t in range(KB):
+            k = KB * (s // GC) + t
+            g.wait_ge(sem["rel%d" % t], got)
+            g.remote_dma(T.b_sb[:, k * F:(k + 1) * F], T.b_rel[t], sem["bin%d" % t], sem.sent, pid, rid, _mask(hop2))
+            sent += len(hop2)
 
     a_total = sum(len(_bits(_a_masks(cores, topo, p)[rank])) for p in range(row * GC, row * GC + GC) if p != rank)
     partner = (rank + GC) % n
@@ -117,9 +122,9 @@ def rank_program(g, core, T, topo):
     te.wait_ge(sem.a_in, a_total)
     for q, k in enumerate(own_k):
         te.matmul(T.acc[:, :], T.a_sb[:, k * 128:(k + 1) * 128], T.b_sb[:, k * F:(k + 1) * F], start=(q == 0), stop=False)
-    te.wait_ge(sem.b_in, b_total)
     for q, k in enumerate(far_k):
         last = q == len(far_k) - 1
+        te.wait_ge(sem["bin%d" % q], b_total)
         ins = te.matmul(T.acc[:, :], T.a_sb[:, k * 128:(k + 1) * 128], T.b_sb[:, k * F:(k + 1) * F], start=False, stop=last)
         if last:
             ins.then_inc(sem.mm, 1)

@@ -13,7 +13,7 @@ SCRATCH = {
 SEMAPHORES = (["ld_a", "ld_b", "a_in", "sent", "mm", "cp", "st"]
               + ["ld_s%d" % t for t in range(KB)] + ["rel%d" % t for t in range(KB)] + ["bin%d" % t for t in range(KB)])
 
-HOP1_ENGINES = 4
+HOP1_ENGINES = 2
 ONCHIP_ENGINES = 4
 
 
@@ -32,19 +32,28 @@ def _same_chip(topo, a, b):
     return topo.host(a) == topo.host(b) and topo.chip(a) == topo.chip(b)
 
 
-def _relays(cores, topo):
+def _relays(cores, topo, t):
     n = len(cores)
     load = [0] * n
     relay = []
     for r in range(n):
         d = (r + GC) % n
+        side = d if t % 2 == 0 else r
         cand = [m for m in range(n) if m != r and m != d
                 and topo.may_write(cores[r], cores[m]) and topo.may_write(cores[m], cores[d])
-                and topo.rack(topo.host(cores[m])) == topo.rack(topo.host(cores[d]))]
+                and topo.rack(topo.host(cores[m])) == topo.rack(topo.host(cores[side]))]
         m = min(cand, key=lambda q: (load[q], q))
         load[m] += 1
         relay.append(m)
     return relay
+
+
+def _hop2_engines(cores, topo, m, d, t):
+    return _bits(topo.mask(cores[m], cores[d]))[t::KB]
+
+
+def _hop1_engines(cores, topo, r, m, t):
+    return _hop2_engines(cores, topo, r, m, t)[:HOP1_ENGINES]
 
 
 def _a_masks(cores, topo, r):
@@ -71,7 +80,7 @@ def rank_program(g, core, T, topo):
     n = len(cores)
     row, col = rank // GC, rank % GC
     sem = T.sem
-    relay = _relays(cores, topo)
+    relay = [_relays(cores, topo, t) for t in range(KB)]
     own_k = [KB * row + t for t in range(KB)]
     far_k = [k for k in range(L) if k not in own_k]
 
@@ -82,10 +91,10 @@ def rank_program(g, core, T, topo):
     g.sync.dma_start(T.b_sb[:, own_k[0] * F:(own_k[-1] + 1) * F], T.b[:, :]).then_inc(sem.ld_b, 16)
 
     sent = 0
-    m = cores[relay[rank]]
-    hop1 = _bits(topo.mask(core, m))[:HOP1_ENGINES]
-    rid, pid = topo.addr(m, core)
     for t in range(KB):
+        m = relay[t][rank]
+        hop1 = _hop1_engines(cores, topo, rank, m, t)
+        rid, pid = topo.addr(cores[m], core)
         g.wait_ge(sem["ld_s%d" % t], 16)
         g.remote_dma(T.b_rel[t], T.b_out[t], sem["rel%d" % t], sem.sent, pid, rid, _mask(hop1))
         sent += len(hop1)
@@ -100,14 +109,14 @@ def rank_program(g, core, T, topo):
     g.wait_ge(sem.ld_a, 16)
     g.remote_dma_fused(transfers, local_sem=sem.sent)
 
-    for s in range(n):
-        if relay[s] != rank:
-            continue
-        d = (s + GC) % n
-        got = len(_bits(topo.mask(cores[s], core))[:HOP1_ENGINES])
-        hop2 = _bits(topo.mask(core, cores[d]))
-        rid, pid = topo.addr(cores[d], core)
-        for t in range(KB):
+    for t in range(KB):
+        for s in range(n):
+            if relay[t][s] != rank:
+                continue
+            d = (s + GC) % n
+            got = len(_hop1_engines(cores, topo, s, rank, t))
+            hop2 = _hop2_engines(cores, topo, rank, d, t)
+            rid, pid = topo.addr(cores[d], core)
             k = KB * (s // GC) + t
             g.wait_ge(sem["rel%d" % t], got)
             g.remote_dma(T.b_sb[:, k * F:(k + 1) * F], T.b_rel[t], sem["bin%d" % t], sem.sent, pid, rid, _mask(hop2))
@@ -115,7 +124,6 @@ def rank_program(g, core, T, topo):
 
     a_total = sum(len(_bits(_a_masks(cores, topo, p)[rank])) for p in range(row * GC, row * GC + GC) if p != rank)
     partner = (rank + GC) % n
-    b_total = len(_bits(topo.mask(cores[relay[partner]], core)))
     te = g.tensor
     te.wait_ge(sem.ld_a, 16)
     te.wait_ge(sem.ld_b, 16)
@@ -124,7 +132,7 @@ def rank_program(g, core, T, topo):
         te.matmul(T.acc[:, :], T.a_sb[:, k * 128:(k + 1) * 128], T.b_sb[:, k * F:(k + 1) * F], start=(q == 0), stop=False)
     for q, k in enumerate(far_k):
         last = q == len(far_k) - 1
-        te.wait_ge(sem["bin%d" % q], b_total)
+        te.wait_ge(sem["bin%d" % q], len(_hop2_engines(cores, topo, relay[q][partner], rank, q)))
         ins = te.matmul(T.acc[:, :], T.a_sb[:, k * 128:(k + 1) * 128], T.b_sb[:, k * F:(k + 1) * F], start=False, stop=last)
         if last:
             ins.then_inc(sem.mm, 1)

from concourse.bass import DstId, RemoteDMATransfer

GR, GC, L, KB, F = 2, 4, 4, 2, 128

SCRATCH = {
    "a_sb": ("sbuf", [128, L * 128], "bfloat16"),
    "b_sb": ("sbuf", [128, L * F], "bfloat16"),
    "b_out": ("dram", [KB, 128, F], "bfloat16"),
    "b_rel": ("dram", [KB, 128, F], "bfloat16"),
    "y_sb": ("sbuf", [128, F], "bfloat16"),
    "acc": ("psum", [128, F], "float32"),
}
SEMAPHORES = (["ld_a", "ld_b", "a_in", "sent", "mm", "cp", "st"]
              + ["ld_s%d" % t for t in range(KB)] + ["rel%d" % t for t in range(KB)] + ["bin%d" % t for t in range(KB)])

HOP1_ENGINES = 2
ONCHIP_ENGINES = 4


def _bits(mask):
    return [e for e in range(16) if (mask >> e) & 1]


def _mask(engines):
    m = 0
    for e in engines:
        m |= 1 << e
    return m


def _same_chip(topo, a, b):
    return topo.host(a) == topo.host(b) and topo.chip(a) == topo.chip(b)


def _relays(cores, topo, t):
    n = len(cores)
    load = [0] * n
    relay = []
    for r in range(n):
        d = (r + GC) % n
        side = d if t % 2 == 0 else r
        cand = [m for m in range(n) if m != r and m != d
                and topo.may_write(cores[r], cores[m]) and topo.may_write(cores[m], cores[d])
                and topo.rack(topo.host(cores[m])) == topo.rack(topo.host(cores[side]))]
        m = min(cand, key=lambda q: (load[q], q))
        load[m] += 1
        relay.append(m)
    return relay


def _hop2_engines(cores, topo, m, d, t):
    return _bits(topo.mask(cores[m], cores[d]))[t::KB]


def _hop1_engines(cores, topo, r, m, t):
    return _hop2_engines(cores, topo, r, m, t)[:HOP1_ENGINES]


def _a_masks(cores, topo, r):
    src = cores[r]
    peers = [p for p in range((r // GC) * GC, (r // GC) * GC + GC) if p != r]
    far = [p for p in peers if not _same_chip(topo, src, cores[p])]
    near = [p for p in peers if _same_chip(topo, src, cores[p])]
    out = {}
    leave = _bits(topo.mask(src, cores[far[0]])) if far else []
    share = len(leave) // max(1, len(far))
    for n, p in enumerate(far):
        out[p] = _mask(leave[n * share:(n + 1) * share])
    for n, p in enumerate(near):
        stay = [e for e in _bits(topo.mask(src, cores[p])) if e not in leave]
        out[p] = _mask(stay[n * ONCHIP_ENGINES:(n + 1) * ONCHIP_ENGINES])
    return out


def rank_program(g, core, T, topo):
    rank = T.rank_of(core)
    if rank is None:
        return
    cores = list(T.cores)
    n = len(cores)
    row, col = rank // GC, rank % GC
    sem = T.sem
    relay = [_relays(cores, topo, t) for t in range(KB)]
    own_k = [KB * row + t for t in range(KB)]
    far_k = [k for k in range(L) if k not in own_k]

    queues = [g.sync, g.scalar]
    for t in range(KB):
        queues[t % 2].dma_start(T.b_out[t], T.b[:, t * F:(t + 1) * F]).then_inc(sem["ld_s%d" % t], 16)
    g.scalar.dma_start(T.a_sb[:, col * 128:(col + 1) * 128], T.a[:, :]).then_inc(sem.ld_a, 16)
    g.sync.dma_start(T.b_sb[:, own_k[0] * F:(own_k[-1] + 1) * F], T.b[:, :]).then_inc(sem.ld_b, 16)

    sent = 0
    for t in range(KB):
        m = relay[t][rank]
        hop1 = _hop1_engines(cores, topo, rank, m, t)
        rid, pid = topo.addr(cores[m], core)
        g.wait_ge(sem["ld_s%d" % t], 16)
        g.remote_dma(T.b_rel[t], T.b_out[t], sem["rel%d" % t], sem.sent, pid, rid, _mask(hop1))
        sent += len(hop1)

    transfers = []
    for p, mask in _a_masks(cores, topo, rank).items():
        rid, pid = topo.addr(cores[p], core)
        blk = T.a_sb[:, col * 128:(col + 1) * 128]
        transfers.append(RemoteDMATransfer(dst_ids=[DstId(rid=rid, pnc=pid)], dma_engine_mask=mask, remote_sem=sem.a_in,
                                           src=blk, dst=blk))
        sent += len(_bits(mask))
    g.wait_ge(sem.ld_a, 16)
    g.remote_dma_fused(transfers, local_sem=sem.sent)

    for t in range(KB):
        for s in range(n):
            if relay[t][s] != rank:
                continue
            d = (s + GC) % n
            got = len(_hop1_engines(cores, topo, s, rank, t))
            hop2 = _hop2_engines(cores, topo, rank, d, t)
            rid, pid = topo.addr(cores[d], core)
            k = KB * (s // GC) + t
            g.wait_ge(sem["rel%d" % t], got)
            g.remote_dma(T.b_sb[:, k * F:(k + 1) * F], T.b_rel[t], sem["bin%d" % t], sem.sent, pid, rid, _mask(hop2))
            sent += len(hop2)

    a_total = sum(len(_bits(_a_masks(cores, topo, p)[rank])) for p in range(row * GC, row * GC + GC) if p != rank)
    partner = (rank + GC) % n
    te = g.tensor
    te.wait_ge(sem.ld_a, 16)
    te.wait_ge(sem.ld_b, 16)
    te.wait_ge(sem.a_in, a_total)
    for q, k in enumerate(own_k):
        te.matmul(T.acc[:, :], T.a_sb[:, k * 128:(k + 1) * 128], T.b_sb[:, k * F:(k + 1) * F], start=(q == 0), stop=False)
    for q, k in enumerate(far_k):
        last = q == len(far_k) - 1
        te.wait_ge(sem["bin%d" % q], len(_hop2_engines(cores, topo, relay[q][partner], rank, q)))
        ins = te.matmul(T.acc[:, :], T.a_sb[:, k * 128:(k + 1) * 128], T.b_sb[:, k * F:(k + 1) * F], start=False, stop=last)
        if last:
            ins.then_inc(sem.mm, 1)

    g.vector.wait_ge(sem.mm, 1)
    g.vector.tensor_copy(T.y_sb[:, :], T.acc[:, :]).then_inc(sem.cp, 1)
    g.sync.wait_ge(sem.cp, 1)
    g.sync.dma_start(T.y[:, :], T.y_sb[:, :]).then_inc(sem.st, 16)
    g.sync.wait_ge(sem.st, 16)
    g.wait_ge(sem.sent, sent)
